import numpy as np
import ml_dtypes


def mxq(x, axis, fmt="e4m3"):
    dtype, down = {"e4m3": (ml_dtypes.float8_e4m3fn, 7), "e5m2": (ml_dtypes.float8_e5m2, 14)}[fmt]
    v = np.moveaxis(np.asarray(x, np.float32).astype(ml_dtypes.bfloat16).astype(np.float64), axis, -1)
    blocks = v.reshape(v.shape[:-1] + (-1, 32))
    amax = np.abs(blocks).max(-1, keepdims=True)
    byte = np.maximum(np.where(amax > 0, np.frexp(amax)[1] - 1 + 127, 0) - down, 1)
    scale = np.exp2(byte - 127.0)
    codes = (blocks / scale).astype(np.float32).astype(dtype).astype(np.float64)
    return np.moveaxis((codes * scale).reshape(v.shape), -1, axis)


WIDE = False


def mx_kscale(k):
    if not WIDE:
        return np.ones(k)
    levels = np.array([10, -10, 5, -5, 0])
    if k % 512:
        return np.exp2(np.random.permutation(np.resize(levels, k // 32))).repeat(32)
    a = np.empty((k // 512, 16))
    for p in range(k // 512):
        a[p, :8] = np.random.permutation(np.resize(levels, 8))
        for g in range(8):
            far = levels[np.abs(levels - a[p, g]) >= 10]
            a[p, g + 8] = far[np.random.randint(len(far))]
    return np.exp2(a.ravel()).repeat(32)


def f64(x):
    return np.asarray(x).astype(np.float64)


def striped(idx):
    return np.tile(idx.reshape(-1, 16).T, (8, 1)).astype(np.uint16)


def unstriped(offs):
    return offs[:16].T.reshape(-1).astype(np.int64)


def pack_weight(w):
    k, n = w.shape
    w = f64(np.asarray(w, np.float32).astype(ml_dtypes.bfloat16)).reshape(k // 32, 32, n)
    amax = np.abs(w).max(1)
    byte = np.clip(np.where(amax > 0, np.frexp(amax)[1] - 1 + 127 - 7, 1), 1, 254)
    scaled = (w * np.exp2(127.0 - byte)[:, None, :]).reshape(k, n).astype(np.float32)
    words = np.ascontiguousarray(scaled.reshape(k // 512, 128, 4, n).transpose(0, 1, 3, 2)).astype(ml_dtypes.float8_e4m3fn).view(np.uint8)
    return words, np.ascontiguousarray(byte.astype(np.uint8).reshape(k // 512, 16, n))


def unpack_weight(words, scales):
    g, p, n, _ = words.shape
    vals = np.ascontiguousarray(words).view(ml_dtypes.float8_e4m3fn).astype(np.float64) * np.repeat(np.exp2(scales.astype(np.float64) - 127.0), 8, axis=1)[..., None]
    return vals.transpose(0, 1, 3, 2).reshape(g * 512, n)


def planes(y):
    n, m = y.shape
    v = y.astype(np.float32).astype(ml_dtypes.bfloat16).astype(np.float64).reshape(n // 32, 32, m)
    top = np.abs(v).max(1)
    byte = np.clip(np.where(top > 0, np.frexp(top)[1] - 1 + 127 - 7, 1), 1, 254)
    codes = (v * np.exp2(127.0 - byte)[:, None, :]).reshape(n, m).astype(np.float32).astype(ml_dtypes.float8_e4m3fn).view(np.uint8)
    words = codes.reshape(n // 512, 128, 4, m).transpose(0, 1, 3, 2)
    return np.ascontiguousarray(words), np.ascontiguousarray(byte.astype(np.uint8).reshape(n // 512, 16, m))


def gelu(v):
    return 0.5 * v * (1.0 + np.tanh(np.sqrt(2.0 / np.pi) * (v + 0.044715 * v**3)))


K, T, S, W, N = 1024, 1024, 512, 1024, 512


def setup_inputs():
    n = np.random.standard_normal
    s = mx_kscale(K)[:, None]
    packed_xT = pack_weight(n((K, T)) * s)
    packed_eT = pack_weight(n((K, W)) * s)
    return {
        "x_words": packed_xT[0],
        "x_scales": packed_xT[1],
        "e_words": packed_eT[0],
        "e_scales": packed_eT[1],
        "w1": (n((K, N)) / np.sqrt(2 * K) / s).astype(np.float32),
        "w2": (n((K, N)) / np.sqrt(2 * K) / s).astype(np.float32),
        "w3": (n((K, N)) / np.sqrt(2 * K) / s).astype(np.float32),
        "w4": (n((K, N)) / np.sqrt(2 * K) / s).astype(np.float32),
        "offs": striped(np.random.permutation(T)[:S]),
        "tok": striped(np.random.permutation(W)[:S]),
    }


def reference(x_words, x_scales, e_words, e_scales, w1, w2, w3, w4, offs, tok):
    xq = unpack_weight(x_words, x_scales)[:, unstriped(offs)]
    e_tok = unpack_weight(e_words, e_scales)[:, unstriped(tok)]
    g = gelu(mxq(f64(w1), 0, "e4m3").T @ xq + mxq(f64(w2), 0, "e4m3").T @ e_tok)
    y = mxq(f64(w3), 0, "e4m3").T @ xq + mxq(f64(w4), 0, "e4m3").T @ e_tok
    out_0 = g * y
    return (out_0,) + planes(out_0)

@@ -1,0 +1,178 @@
+from contextlib import ExitStack
+
+import concourse.mybir as mybir
+
+K, T, S, N = 1024, 1024, 512, 512
+FLOPS = 2 * 4 * K * N * S
+
+F32 = mybir.dt.float32
+BF16 = mybir.dt.bfloat16
+I32 = mybir.dt.int32
+U32 = mybir.dt.uint32
+U16 = mybir.dt.uint16
+U8 = mybir.dt.uint8
+FP8X4 = mybir.dt.float8_e4m3fn_x4
+GELU = mybir.ActivationFunctionType.Gelu_apprx_tanh
+MULT = mybir.AluOpType.mult
+
+P = 128
+PACK = 4
+K_PASS = P * PACK
+PASSES = K // K_PASS
+QUADS = 4
+CHUNKS = ((0, 256), (256, 384), (384, 512))
+LAST_SPLIT = 384
+
+
+def tile_picked_zmtp_gelu_po_kernel(
+    tc, x_words, x_scales, e_words, e_scales, w1, w2, w3, w4, offs, tok, out_0, out_1, out_2
+):
+    nc = tc.nc
+    with ExitStack() as ctx:
+        keep = ctx.enter_context(tc.tile_pool(name="keep", bufs=1))
+        psum = ctx.enter_context(tc.psum_pool(name="psum", bufs=1))
+
+        def sb(name, shape, dtype):
+            return keep.tile(shape, dtype, name=name, align_bytes=64)
+
+        tables = {"x": (x_words, x_scales, offs, 0), "e": (e_words, e_scales, tok, 8)}
+        lists = {name: keep.tile([P, S // 16], U16, name="list_" + name) for name in tables}
+
+        pieces = [
+            (w, table, product, g)
+            for w, table, product in ((w1, "x", "gate"), (w2, "e", "gate"), (w3, "x", "value"), (w4, "e", "value"))
+            for g in range(PASSES)
+        ]
+        spans = [[(0, N)] for piece in pieces]
+        spans[-1] = [(0, LAST_SPLIT), (LAST_SPLIT, N)]
+        raw = [
+            [sb("raw%d_%d" % (i, c0), [P, PACK, c1 - c0], F32) for c0, c1 in spans[i]] for i in range(len(pieces))
+        ]
+        table_words = {(n, g): sb("words_%s%d" % (n, g), [P, T], I32) for n in tables for g in range(PASSES)}
+        table_scales = {n: sb("scales_" + n, [P, T], U8) for n in tables}
+        picked_words = {(n, g): sb("picked_words_%s%d" % (n, g), [P, S], U32) for n in tables for g in range(PASSES)}
+        picked_scales = {n: sb("picked_scales_" + n, [P, S], U8) for n in tables}
+
+        for n in tables:
+            nc.vector.memset(table_scales[n][:].bitcast(I32), 0)
+
+        def load_scales(n):
+            for q in range(QUADS):
+                row = 32 * q + tables[n][3]
+                nc.sync.dma_start(
+                    out=table_scales[n][row : row + 4 * PASSES, :].bitcast(I32),
+                    in_=tables[n][1][:, 4 * q : 4 * q + 4, :].bitcast(I32),
+                )
+            nc.sync.dma_start(lists[n][:], tables[n][2])
+
+        for i, (w, table, product, g) in enumerate(pieces):
+            rows = w[g * K_PASS : (g + 1) * K_PASS, :]
+            for tile, (c0, c1) in zip(raw[i], spans[i]):
+                nc.sync.dma_start(out=tile[:], in_=rows[:, c0:c1].rearrange("(p j) c -> p j c", j=PACK))
+            if i == 0:
+                load_scales("x")
+            if product == "gate":
+                nc.sync.dma_start(
+                    out=table_words[table, g][:],
+                    in_=tables[table][0][g].rearrange("p n t -> p (n t)").bitcast(I32),
+                )
+            if i == 1:
+                load_scales("e")
+
+        acc = {
+            (product, t): psum.tile([P, S], F32, name="acc_%s%d" % (product, t))
+            for product in ("gate", "value")
+            for t in range(PACK)
+        }
+        gate = [sb("gate%d" % t, [P, S], F32) for t in range(PACK)]
+
+        for i, (w, table, product, g) in enumerate(pieces):
+            last = i == len(pieces) - 1
+            rounded = [sb("rounded%d_%d" % (i, u), [P, 2, P, PACK], BF16) for u in range(2)]
+            for tile, (c0, c1) in zip(raw[i], spans[i]):
+                for u in range(2):
+                    src = tile[:].rearrange("p j (m t) -> p m j t", t=PACK)[:, :, :, 2 * u : 2 * u + 2]
+                    dst = rounded[u][:, :, c0 // PACK : c1 // PACK, :].rearrange("p t m j -> p m j t")
+                    if u == 0 and i not in (0, 2):
+                        nc.vector.tensor_copy(out=dst, in_=src)
+                    else:
+                        nc.scalar.copy(out=dst, in_=src)
+            if product == "gate":
+                nc.vector.tensor_copy(
+                    out=picked_words[table, g][:],
+                    in_=table_words[table, g][:].bitcast(U32).indirect(lists[table][:]),
+                )
+                if g == 0:
+                    nc.vector.tensor_copy(
+                        out=picked_scales[table][:],
+                        in_=table_scales[table][:].indirect(lists[table][:]),
+                    )
+            plane = tables[table][3] + 4 * g
+            for u in range(2):
+                codes = sb("codes%d_%d" % (i, u), [P, 2 * P], U32)
+                scales = sb("wscales%d_%d" % (i, u), [P, 2 * P], U8)
+                flat = rounded[u][:].rearrange("p t m j -> p (t m j)")
+                if last:
+                    for v in range(2):
+                        nc.vector.quantize_mx(
+                            out=codes[:, v * P : (v + 1) * P].bitcast(FP8X4),
+                            scales=scales[:, v * P : (v + 1) * P],
+                            in_=flat[:, v * K_PASS : (v + 1) * K_PASS],
+                        )
+                else:
+                    nc.vector.quantize_mx(out=codes[:].bitcast(FP8X4), scales=scales[:], in_=flat)
+                for v in range(2):
+                    nc.tensor.matmul_mx(
+                        out=acc[product, 2 * u + v][:],
+                        lhsT=codes[:, v * P : (v + 1) * P].bitcast(FP8X4),
+                        lhsT_scale=scales[:, v * P : (v + 1) * P],
+                        rhs=picked_words[table, g][:].bitcast(FP8X4),
+                        rhs_scale=picked_scales[table][plane:, :],
+                        start=(i % 4 == 0),
+                        stop=(i % 4 == 3),
+                    )
+            if i == 3:
+                for t in range(PACK):
+                    nc.scalar.activation(out=gate[t][:], in_=acc["gate", t][:], func=GELU)
+
+        out_rows = out_0.rearrange("(p t) c -> p t c", t=PACK)
+        out_codes = sb("out_codes", [P, S], U32)
+        out_scales = sb("out_scales", [P, S], U8)
+        words_out = out_1[0].rearrange("p n t -> p (n t)").bitcast(I32)
+        results, packed = [], []
+        for c, (c0, c1) in enumerate(CHUNKS):
+            result = sb("result%d" % c, [P, PACK, c1 - c0], F32)
+            for t in range(PACK):
+                nc.vector.tensor_tensor(
+                    out=result[:, t, :], in0=acc["value", t][:, c0:c1], in1=gate[t][:, c0:c1], op=MULT
+                )
+                if c == 0 and t % 2 == 1:
+                    nc.sync.dma_start(out=out_rows[:, t - 1 : t + 1, c0:c1], in_=result[:, t - 1 : t + 1, :])
+            if c > 0:
+                nc.sync.dma_start(out=out_rows[:, :, c0:c1], in_=result[:])
+            results.append(result)
+        for c, (c0, c1) in enumerate(CHUNKS):
+            side = sb("side%d" % c, [P, c1 - c0, PACK], BF16)
+            src = results[c][:].rearrange("p t (a i) -> p a t i", i=4)
+            dst = side[:].rearrange("p (a i) t -> p a t i", i=4)
+            if c < len(CHUNKS) - 1:
+                nc.scalar.copy(out=dst, in_=src)
+            else:
+                nc.vector.tensor_copy(out=dst, in_=src)
+            packed.append(side)
+        for c, (c0, c1) in enumerate(CHUNKS):
+            nc.vector.quantize_mx(
+                out=out_codes[:, c0:c1].bitcast(FP8X4),
+                scales=out_scales[:, c0:c1],
+                in_=packed[c][:].rearrange("p n t -> p (n t)"),
+            )
+            if c == 0:
+                nc.sync.dma_start(out=words_out[:, c0:c1], in_=out_codes[:, c0:c1].bitcast(I32))
+        c0 = CHUNKS[1][0]
+        nc.sync.dma_start(out=words_out[:, c0:], in_=out_codes[:, c0:].bitcast(I32))
+        for q in range(QUADS):
+            queue = nc.sync if q % 2 == 0 else nc.scalar
+            queue.dma_start(
+                out=out_2[0, 4 * q : 4 * q + 4, :].bitcast(I32),
+                in_=out_scales[32 * q : 32 * q + 4, :].bitcast(I32),
+            )

@@ -32,8 +32,8 @@ def tile_picked_zmtp_gelu_po_kernel(
         keep = ctx.enter_context(tc.tile_pool(name="keep", bufs=1))
         psum = ctx.enter_context(tc.psum_pool(name="psum", bufs=1))
 
-        def sb(name, shape, dtype):
-            return keep.tile(shape, dtype, name=name, align_bytes=64)
+        def sb(name, shape, dtype, tag=""):
+            return keep.tile(shape, dtype, name=name, tag=tag or name, align_bytes=64)
 
         tables = {"x": (x_words, x_scales, offs, 0), "e": (e_words, e_scales, tok, 8)}
         lists = {name: keep.tile([P, S // 16], U16, name="list_" + name) for name in tables}
@@ -51,33 +51,37 @@ def tile_picked_zmtp_gelu_po_kernel(
         table_words = {(n, g): sb("words_%s%d" % (n, g), [P, T], I32) for n in tables for g in range(PASSES)}
         table_scales = {n: sb("scales_" + n, [P, T], U8) for n in tables}
         picked_words = {(n, g): sb("picked_words_%s%d" % (n, g), [P, S], U32) for n in tables for g in range(PASSES)}
-        picked_scales = {n: sb("picked_scales_" + n, [P, S], U8) for n in tables}
+        picked_scales = {}
 
-        for n in tables:
-            nc.vector.memset(table_scales[n][:].bitcast(I32), 0)
+        nc.gpsimd.memset(table_scales["x"][:].bitcast(I32), 0)
+        nc.vector.memset(table_scales["e"][:].bitcast(I32), 0)
+        warm = sb("warm", [P, 2], F32)
+        nc.vector.memset(warm[:, 0:1], 0.0)
+        nc.scalar.activation(out=warm[:, 1:2], in_=warm[:, 0:1], func=GELU)
 
         def load_scales(n):
             for q in range(QUADS):
                 row = 32 * q + tables[n][3]
-                nc.sync.dma_start(
+                nc.gpsimd.dma_start(
                     out=table_scales[n][row : row + 4 * PASSES, :].bitcast(I32),
                     in_=tables[n][1][:, 4 * q : 4 * q + 4, :].bitcast(I32),
                 )
-            nc.sync.dma_start(lists[n][:], tables[n][2])
+
+        for n in tables:
+            load_scales(n)
 
         for i, (w, table, product, g) in enumerate(pieces):
             rows = w[g * K_PASS : (g + 1) * K_PASS, :]
             for tile, (c0, c1) in zip(raw[i], spans[i]):
                 nc.sync.dma_start(out=tile[:], in_=rows[:, c0:c1].rearrange("(p j) c -> p j c", j=PACK))
             if i == 0:
-                load_scales("x")
+                for n in tables:
+                    nc.sync.dma_start(lists[n][:], tables[n][2])
             if product == "gate":
                 nc.sync.dma_start(
                     out=table_words[table, g][:],
                     in_=tables[table][0][g].rearrange("p n t -> p (n t)").bitcast(I32),
                 )
-            if i == 1:
-                load_scales("e")
 
         acc = {
             (product, t): psum.tile([P, S], F32, name="acc_%s%d" % (product, t))
@@ -102,12 +106,8 @@ def tile_picked_zmtp_gelu_po_kernel(
                     out=picked_words[table, g][:],
                     in_=table_words[table, g][:].bitcast(U32).indirect(lists[table][:]),
                 )
-                if g == 0:
-                    nc.vector.tensor_copy(
-                        out=picked_scales[table][:],
-                        in_=table_scales[table][:].indirect(lists[table][:]),
-                    )
             plane = tables[table][3] + 4 * g
+            quantised = []
             for u in range(2):
                 codes = sb("codes%d_%d" % (i, u), [P, 2 * P], U32)
                 scales = sb("wscales%d_%d" % (i, u), [P, 2 * P], U8)
@@ -121,16 +121,25 @@ def tile_picked_zmtp_gelu_po_kernel(
                         )
                 else:
                     nc.vector.quantize_mx(out=codes[:].bitcast(FP8X4), scales=scales[:], in_=flat)
-                for v in range(2):
-                    nc.tensor.matmul_mx(
-                        out=acc[product, 2 * u + v][:],
-                        lhsT=codes[:, v * P : (v + 1) * P].bitcast(FP8X4),
-                        lhsT_scale=scales[:, v * P : (v + 1) * P],
-                        rhs=picked_words[table, g][:].bitcast(FP8X4),
-                        rhs_scale=picked_scales[table][plane:, :],
-                        start=(i % 4 == 0),
-                        stop=(i % 4 == 3),
-                    )
+                quantised.append((codes, scales))
+            if product == "gate" and g == 0:
+                picked_scales[table] = sb("picked_scales_" + table, [P, S], U8, tag="rounded%d_0" % (i // 2))
+                nc.vector.tensor_copy(
+                    out=picked_scales[table][:],
+                    in_=table_scales[table][:].indirect(lists[table][:]),
+                )
+            for t in range(PACK):
+                codes, scales = quantised[t // 2]
+                cols = slice((t % 2) * P, (t % 2 + 1) * P)
+                nc.tensor.matmul_mx(
+                    out=acc[product, t][:],
+                    lhsT=codes[:, cols].bitcast(FP8X4),
+                    lhsT_scale=scales[:, cols],
+                    rhs=picked_words[table, g][:].bitcast(FP8X4),
+                    rhs_scale=picked_scales[table][plane:, :],
+                    start=(i % 4 == 0),
+                    stop=(i % 4 == 3),
+                )
             if i == 3:
                 for t in range(PACK):
                     nc.scalar.activation(out=gate[t][:], in_=acc["gate", t][:], func=GELU)

@@ -22,6 +22,7 @@ PASSES = K // K_PASS
 QUADS = 4
 CHUNKS = ((0, 256), (256, 384), (384, 512))
 LAST_SPLIT = 384
+GELU_AFTER = {4: ((0, "raw4_0"), (1, "rounded4_1")), 5: ((2, "raw5_0"),), 6: ((3, "raw6_0"),)}
 
 
 def tile_picked_zmtp_gelu_po_kernel(
@@ -46,9 +47,10 @@ def tile_picked_zmtp_gelu_po_kernel(
         spans = [[(0, N)] for piece in pieces]
         spans[-1] = [(0, LAST_SPLIT), (LAST_SPLIT, N)]
         raw = [
-            [sb("raw%d_%d" % (i, c0), [P, PACK, c1 - c0], F32) for c0, c1 in spans[i]] for i in range(len(pieces))
+            [sb("raw%d_%d" % (i, c0), [P, PACK, c1 - c0], F32)[:] for c0, c1 in spans[i]]
+            for i in range(len(pieces))
         ]
-        table_words = {(n, g): sb("words_%s%d" % (n, g), [P, T], I32) for n in tables for g in range(PASSES)}
+        table_words = {n: sb("words_" + n, [P, PASSES, T], I32) for n in tables}
         table_scales = {n: sb("scales_" + n, [P, T], U8) for n in tables}
         picked_words = {(n, g): sb("picked_words_%s%d" % (n, g), [P, S], U32) for n in tables for g in range(PASSES)}
         picked_scales = {}
@@ -71,41 +73,39 @@ def tile_picked_zmtp_gelu_po_kernel(
             load_scales(n)
 
         for i, (w, table, product, g) in enumerate(pieces):
+            if product == "gate" and g == 0:
+                nc.sync.dma_start(
+                    out=table_words[table][:],
+                    in_=tables[table][0].rearrange("g p n t -> p g (n t)").bitcast(I32),
+                )
+                nc.sync.dma_start(lists[table][:], tables[table][2])
             rows = w[g * K_PASS : (g + 1) * K_PASS, :]
             for tile, (c0, c1) in zip(raw[i], spans[i]):
-                nc.sync.dma_start(out=tile[:], in_=rows[:, c0:c1].rearrange("(p j) c -> p j c", j=PACK))
-            if i == 0:
-                for n in tables:
-                    nc.sync.dma_start(lists[n][:], tables[n][2])
-            if product == "gate":
-                nc.sync.dma_start(
-                    out=table_words[table, g][:],
-                    in_=tables[table][0][g].rearrange("p n t -> p (n t)").bitcast(I32),
-                )
+                nc.sync.dma_start(out=tile, in_=rows[:, c0:c1].rearrange("(p j) c -> p j c", j=PACK))
 
         acc = {
             (product, t): psum.tile([P, S], F32, name="acc_%s%d" % (product, t))
             for product in ("gate", "value")
             for t in range(PACK)
         }
-        gate = [sb("gate%d" % t, [P, S], F32) for t in range(PACK)]
+        gate = []
 
         for i, (w, table, product, g) in enumerate(pieces):
             last = i == len(pieces) - 1
-            rounded = [sb("rounded%d_%d" % (i, u), [P, 2, P, PACK], BF16) for u in range(2)]
-            for tile, (c0, c1) in zip(raw[i], spans[i]):
-                for u in range(2):
-                    src = tile[:].rearrange("p j (m t) -> p m j t", t=PACK)[:, :, :, 2 * u : 2 * u + 2]
-                    dst = rounded[u][:, :, c0 // PACK : c1 // PACK, :].rearrange("p t m j -> p m j t")
-                    if u == 0 and i not in (0, 2):
-                        nc.vector.tensor_copy(out=dst, in_=src)
-                    else:
-                        nc.scalar.copy(out=dst, in_=src)
             if product == "gate":
                 nc.vector.tensor_copy(
                     out=picked_words[table, g][:],
-                    in_=table_words[table, g][:].bitcast(U32).indirect(lists[table][:]),
+                    in_=table_words[table][:, g, :].bitcast(U32).indirect(lists[table][:]),
                 )
+            rounded = [sb("rounded%d_%d" % (i, u), [P, 2, P, PACK], BF16) for u in range(2)]
+            for tile, (c0, c1) in zip(raw[i], spans[i]):
+                for u in range(2):
+                    src = tile.rearrange("p j (m t) -> p m j t", t=PACK)[:, :, :, 2 * u : 2 * u + 2]
+                    dst = rounded[u][:, :, c0 // PACK : c1 // PACK, :].rearrange("p t m j -> p m j t")
+                    if u == 0 and i >= 3:
+                        nc.vector.tensor_copy(out=dst, in_=src)
+                    else:
+                        nc.scalar.copy(out=dst, in_=src)
             plane = tables[table][3] + 4 * g
             quantised = []
             for u in range(2):
@@ -123,7 +123,7 @@ def tile_picked_zmtp_gelu_po_kernel(
                     nc.vector.quantize_mx(out=codes[:].bitcast(FP8X4), scales=scales[:], in_=flat)
                 quantised.append((codes, scales))
             if product == "gate" and g == 0:
-                picked_scales[table] = sb("picked_scales_" + table, [P, S], U8, tag="rounded%d_0" % (i // 2))
+                picked_scales[table] = sb("picked_scales_" + table, [P, S], U8, tag="rounded1_1" if i else "")
                 nc.vector.tensor_copy(
                     out=picked_scales[table][:],
                     in_=table_scales[table][:].indirect(lists[table][:]),
@@ -140,9 +140,9 @@ def tile_picked_zmtp_gelu_po_kernel(
                     start=(i % 4 == 0),
                     stop=(i % 4 == 3),
                 )
-            if i == 3:
-                for t in range(PACK):
-                    nc.scalar.activation(out=gate[t][:], in_=acc["gate", t][:], func=GELU)
+            for t, tag in GELU_AFTER.get(i, ()):
+                gate.append(sb("gate%d" % t, [P, S], F32, tag=tag))
+                nc.scalar.activation(out=gate[t][:], in_=acc["gate", t][:], func=GELU)
 
         out_rows = out_0.rearrange("(p t) c -> p t c", t=PACK)
         out_codes = sb("out_codes", [P, S], U32)

@@ -22,7 +22,7 @@ PASSES = K // K_PASS
 QUADS = 4
 CHUNKS = ((0, 256), (256, 384), (384, 512))
 LAST_SPLIT = 384
-GELU_AFTER = {4: ((0, "raw4_0"), (1, "rounded4_1")), 5: ((2, "raw5_0"),), 6: ((3, "raw6_0"),)}
+GELU_AFTER = {4: ((0, "raw4_0"),), 5: ((1, "raw5_0"),), 6: ((2, "raw6_0"),), 7: ((3, "raw7_384"),)}
 
 
 def tile_picked_zmtp_gelu_po_kernel(
@@ -123,7 +123,7 @@ def tile_picked_zmtp_gelu_po_kernel(
                     nc.vector.quantize_mx(out=codes[:].bitcast(FP8X4), scales=scales[:], in_=flat)
                 quantised.append((codes, scales))
             if product == "gate" and g == 0:
-                picked_scales[table] = sb("picked_scales_" + table, [P, S], U8, tag="rounded1_1" if i else "")
+                picked_scales[table] = sb("picked_scales_" + table, [P, S], U8, tag="rounded%d_1" % (i // 2))
                 nc.vector.tensor_copy(
                     out=picked_scales[table][:],
                     in_=table_scales[table][:].indirect(lists[table][:]),

@@ -20,9 +20,11 @@ PACK = 4
 K_PASS = P * PACK
 PASSES = K // K_PASS
 QUADS = 4
-CHUNKS = ((0, 256), (256, 384), (384, 512))
-LAST_SPLIT = 384
-GELU_AFTER = {4: ((0, "raw4_0"),), 5: ((1, "raw5_0"),), 6: ((2, "raw6_0"),), 7: ((3, "raw7_384"),)}
+HALF = S // 2
+STORE_AFTER = ((1, 2, 4), (2, 4))
+LAST_CAST = 44
+VALUE_SHARES = ((128,), (152,), (152,), (172,))
+LAST_SPANS = ((0, 512),)
 
 
 def tile_picked_zmtp_gelu_po_kernel(
@@ -38,18 +40,6 @@ def tile_picked_zmtp_gelu_po_kernel(
 
         tables = {"x": (x_words, x_scales, offs, 0), "e": (e_words, e_scales, tok, 8)}
         lists = {name: keep.tile([P, S // 16], U16, name="list_" + name) for name in tables}
-
-        pieces = [
-            (w, table, product, g)
-            for w, table, product in ((w1, "x", "gate"), (w2, "e", "gate"), (w3, "x", "value"), (w4, "e", "value"))
-            for g in range(PASSES)
-        ]
-        spans = [[(0, N)] for piece in pieces]
-        spans[-1] = [(0, LAST_SPLIT), (LAST_SPLIT, N)]
-        raw = [
-            [sb("raw%d_%d" % (i, c0), [P, PACK, c1 - c0], F32)[:] for c0, c1 in spans[i]]
-            for i in range(len(pieces))
-        ]
         table_words = {n: sb("words_" + n, [P, PASSES, T], I32) for n in tables}
         table_scales = {n: sb("scales_" + n, [P, T], U8) for n in tables}
         picked_words = {(n, g): sb("picked_words_%s%d" % (n, g), [P, S], U32) for n in tables for g in range(PASSES)}
@@ -69,50 +59,64 @@ def tile_picked_zmtp_gelu_po_kernel(
                     in_=tables[n][1][:, 4 * q : 4 * q + 4, :].bitcast(I32),
                 )
 
-        for n in tables:
-            load_scales(n)
+        def load_table(n):
+            nc.sync.dma_start(
+                out=table_words[n][:],
+                in_=tables[n][0].rearrange("g p n t -> p g (n t)").bitcast(I32),
+            )
+            nc.sync.dma_start(lists[n][:], tables[n][2])
 
-        for i, (w, table, product, g) in enumerate(pieces):
-            if product == "gate" and g == 0:
-                nc.sync.dma_start(
-                    out=table_words[table][:],
-                    in_=tables[table][0].rearrange("g p n t -> p g (n t)").bitcast(I32),
-                )
-                nc.sync.dma_start(lists[table][:], tables[table][2])
-            rows = w[g * K_PASS : (g + 1) * K_PASS, :]
-            for tile, (c0, c1) in zip(raw[i], spans[i]):
-                nc.sync.dma_start(out=tile, in_=rows[:, c0:c1].rearrange("(p j) c -> p j c", j=PACK))
+        raw = {}
 
-        acc = {
-            (product, t): psum.tile([P, S], F32, name="acc_%s%d" % (product, t))
-            for product in ("gate", "value")
-            for t in range(PACK)
-        }
-        gate = []
+        def load_pass(name, w, g, spans):
+            rows = w[g * K_PASS : (g + 1) * K_PASS, :].rearrange("(p j) c -> p j c", j=PACK)
+            raw[name, g] = []
+            for c0, c1 in spans:
+                tile = sb("raw_%s%d_%d" % (name, g, c0), [P, PACK, c1 - c0], F32)
+                nc.sync.dma_start(out=tile[:], in_=rows[:, :, c0:c1])
+                raw[name, g].append((tile[:], c0, c1))
 
-        for i, (w, table, product, g) in enumerate(pieces):
-            last = i == len(pieces) - 1
-            if product == "gate":
-                nc.vector.tensor_copy(
-                    out=picked_words[table, g][:],
-                    in_=table_words[table][:, g, :].bitcast(U32).indirect(lists[table][:]),
-                )
-            rounded = [sb("rounded%d_%d" % (i, u), [P, 2, P, PACK], BF16) for u in range(2)]
-            for tile, (c0, c1) in zip(raw[i], spans[i]):
+        load_scales("x")
+        load_scales("e")
+        load_table("x")
+        load_pass("w1", w1, 0, ((0, N),))
+        load_pass("w1", w1, 1, ((0, N),))
+        load_table("e")
+        load_pass("w2", w2, 0, ((0, N),))
+        load_pass("w2", w2, 1, ((0, N),))
+        load_pass("w3", w3, 0, ((0, N),))
+        load_pass("w3", w3, 1, ((0, N),))
+        load_pass("w4", w4, 0, ((0, N),))
+        load_pass("w4", w4, 1, LAST_SPANS)
+
+        def gather_words(n, g):
+            nc.vector.tensor_copy(
+                out=picked_words[n, g][:],
+                in_=table_words[n][:, g, :].bitcast(U32).indirect(lists[n][:]),
+            )
+
+        def gather_scales(n, tag):
+            picked_scales[n] = sb("picked_scales_" + n, [P, S], U8, tag=tag)
+            nc.vector.tensor_copy(out=picked_scales[n][:], in_=table_scales[n][:].indirect(lists[n][:]))
+
+        def quantise(name, g, on_vector, narrow=False):
+            rounded = [sb("rounded_%s%d_%d" % (name, g, u), [P, 2, P, PACK], BF16) for u in range(2)]
+            for (tile, c0, c1), share in zip(raw[name, g], on_vector):
                 for u in range(2):
                     src = tile.rearrange("p j (m t) -> p m j t", t=PACK)[:, :, :, 2 * u : 2 * u + 2]
                     dst = rounded[u][:, :, c0 // PACK : c1 // PACK, :].rearrange("p t m j -> p m j t")
-                    if u == 0 and i >= 3:
-                        nc.vector.tensor_copy(out=dst, in_=src)
-                    else:
-                        nc.scalar.copy(out=dst, in_=src)
-            plane = tables[table][3] + 4 * g
-            quantised = []
+                    width = (c1 - c0) // PACK
+                    cut = min(max(share - u * width, 0), width)
+                    if cut > 0:
+                        nc.vector.tensor_copy(out=dst[:, :cut], in_=src[:, :cut])
+                    if cut < width:
+                        nc.scalar.copy(out=dst[:, cut:], in_=src[:, cut:])
+            operands = []
             for u in range(2):
-                codes = sb("codes%d_%d" % (i, u), [P, 2 * P], U32)
-                scales = sb("wscales%d_%d" % (i, u), [P, 2 * P], U8)
+                codes = sb("codes_%s%d_%d" % (name, g, u), [P, 2 * P], U32)
+                scales = sb("wscales_%s%d_%d" % (name, g, u), [P, 2 * P], U8)
                 flat = rounded[u][:].rearrange("p t m j -> p (t m j)")
-                if last:
+                if narrow:
                     for v in range(2):
                         nc.vector.quantize_mx(
                             out=codes[:, v * P : (v + 1) * P].bitcast(FP8X4),
@@ -121,64 +125,89 @@ def tile_picked_zmtp_gelu_po_kernel(
                         )
                 else:
                     nc.vector.quantize_mx(out=codes[:].bitcast(FP8X4), scales=scales[:], in_=flat)
-                quantised.append((codes, scales))
-            if product == "gate" and g == 0:
-                picked_scales[table] = sb("picked_scales_" + table, [P, S], U8, tag="rounded%d_1" % (i // 2))
-                nc.vector.tensor_copy(
-                    out=picked_scales[table][:],
-                    in_=table_scales[table][:].indirect(lists[table][:]),
-                )
-            for t in range(PACK):
-                codes, scales = quantised[t // 2]
-                cols = slice((t % 2) * P, (t % 2 + 1) * P)
-                nc.tensor.matmul_mx(
-                    out=acc[product, t][:],
-                    lhsT=codes[:, cols].bitcast(FP8X4),
-                    lhsT_scale=scales[:, cols],
-                    rhs=picked_words[table, g][:].bitcast(FP8X4),
-                    rhs_scale=picked_scales[table][plane:, :],
-                    start=(i % 4 == 0),
-                    stop=(i % 4 == 3),
-                )
-            for t, tag in GELU_AFTER.get(i, ()):
-                gate.append(sb("gate%d" % t, [P, S], F32, tag=tag))
-                nc.scalar.activation(out=gate[t][:], in_=acc["gate", t][:], func=GELU)
+                for v in range(2):
+                    operands.append((codes[:, v * P : (v + 1) * P], scales[:, v * P : (v + 1) * P]))
+            return operands
+
+        def multiply(acc, operand, n, g, c0, c1, start, stop):
+            plane = tables[n][3] + 4 * g
+            nc.tensor.matmul_mx(
+                out=acc,
+                lhsT=operand[0].bitcast(FP8X4),
+                lhsT_scale=operand[1],
+                rhs=picked_words[n, g][:, c0:c1].bitcast(FP8X4),
+                rhs_scale=picked_scales[n][plane:, c0:c1],
+                start=start,
+                stop=stop,
+            )
+
+        bank = {(h, t): psum.tile([P, 2, HALF], F32, name="bank%d%d" % (h, t)) for h in range(2) for t in range(PACK)}
+        gate = {}
+
+        def products(operands, side, n, g, start, stop):
+            for h in range(2):
+                for t in range(PACK):
+                    multiply(bank[h, t][:, side, :], operands[t], n, g, h * HALF, (h + 1) * HALF, start, stop)
+
+        def gelu(h, slots, tag):
+            tile = sb("gate%d%d" % (h, slots[0]), [P, len(slots), HALF], F32, tag=tag)
+            for i, t in enumerate(slots):
+                gate[h, t] = tile[:, i, :]
+                nc.scalar.activation(out=gate[h, t], in_=bank[h, t][:, 0, :], func=GELU)
+
+        gate_pieces = (("w1", "x", 0), ("w1", "x", 1), ("w2", "e", 0), ("w2", "e", 1))
+        for i, (name, n, g) in enumerate(gate_pieces):
+            gather_words(n, g)
+            operands = quantise(name, g, (P * (i // 2),))
+            if g == 0:
+                gather_scales(n, ("rounded_w10_1", "rounded_w20_0")[i // 2])
+            products(operands, 0, n, g, i == 0, i == 3)
+        value_pieces = (("w3", "x", 0), ("w3", "x", 1), ("w4", "e", 0), ("w4", "e", 1))
+        for i, (name, n, g) in enumerate(value_pieces):
+            operands = quantise(name, g, VALUE_SHARES[i], narrow=i == 3)
+            if i in (1, 2):
+                gelu(0, (2 * i - 2, 2 * i - 1), "raw_%s%d_0" % (name, g))
+            if i == 3:
+                gelu(1, (0, 1, 2, 3), "raw_w41_0")
+            products(operands, 1, n, g, i == 0, i == 3)
 
         out_rows = out_0.rearrange("(p t) c -> p t c", t=PACK)
         out_codes = sb("out_codes", [P, S], U32)
         out_scales = sb("out_scales", [P, S], U8)
         words_out = out_1[0].rearrange("p n t -> p (n t)").bitcast(I32)
-        results, packed = [], []
-        for c, (c0, c1) in enumerate(CHUNKS):
-            result = sb("result%d" % c, [P, PACK, c1 - c0], F32)
-            for t in range(PACK):
-                nc.vector.tensor_tensor(
-                    out=result[:, t, :], in0=acc["value", t][:, c0:c1], in1=gate[t][:, c0:c1], op=MULT
-                )
-                if c == 0 and t % 2 == 1:
-                    nc.sync.dma_start(out=out_rows[:, t - 1 : t + 1, c0:c1], in_=result[:, t - 1 : t + 1, :])
-            if c > 0:
-                nc.sync.dma_start(out=out_rows[:, :, c0:c1], in_=result[:])
-            results.append(result)
-        for c, (c0, c1) in enumerate(CHUNKS):
-            side = sb("side%d" % c, [P, c1 - c0, PACK], BF16)
-            src = results[c][:].rearrange("p t (a i) -> p a t i", i=4)
-            dst = side[:].rearrange("p (a i) t -> p a t i", i=4)
-            if c < len(CHUNKS) - 1:
-                nc.scalar.copy(out=dst, in_=src)
-            else:
-                nc.vector.tensor_copy(out=dst, in_=src)
-            packed.append(side)
-        for c, (c0, c1) in enumerate(CHUNKS):
+        results = [sb("result%d" % h, [P, PACK, HALF], F32) for h in range(2)]
+        sides = [sb("side%d" % h, [P, HALF, PACK], BF16) for h in range(2)]
+
+        def cast(engine_copy, h, a0, a1):
+            src = results[h][:].rearrange("p t (a i) -> p a t i", i=4)
+            dst = sides[h][:].rearrange("p (a i) t -> p a t i", i=4)
+            engine_copy(out=dst[:, a0:a1], in_=src[:, a0:a1])
+
+        def quantise_result(h, c0, c1):
             nc.vector.quantize_mx(
-                out=out_codes[:, c0:c1].bitcast(FP8X4),
-                scales=out_scales[:, c0:c1],
-                in_=packed[c][:].rearrange("p n t -> p (n t)"),
+                out=out_codes[:, h * HALF + c0 : h * HALF + c1].bitcast(FP8X4),
+                scales=out_scales[:, h * HALF + c0 : h * HALF + c1],
+                in_=sides[h][:, c0:c1, :].rearrange("p n t -> p (n t)"),
             )
-            if c == 0:
-                nc.sync.dma_start(out=words_out[:, c0:c1], in_=out_codes[:, c0:c1].bitcast(I32))
-        c0 = CHUNKS[1][0]
-        nc.sync.dma_start(out=words_out[:, c0:], in_=out_codes[:, c0:].bitcast(I32))
+
+        for h in range(2):
+            cols = slice(h * HALF, (h + 1) * HALF)
+            stored = 0
+            for t in range(PACK):
+                nc.vector.tensor_tensor(out=results[h][:, t, :], in0=bank[h, t][:, 1, :], in1=gate[h, t], op=MULT)
+                if t + 1 in STORE_AFTER[h]:
+                    nc.sync.dma_start(out=out_rows[:, stored : t + 1, cols], in_=results[h][:, stored : t + 1, :])
+                    stored = t + 1
+            if h == 0:
+                cast(nc.scalar.copy, 0, 0, 32)
+                cast(nc.scalar.copy, 0, 32, 64)
+        cast(nc.scalar.copy, 1, LAST_CAST, 64)
+        quantise_result(0, 0, 128)
+        cast(nc.vector.tensor_copy, 1, 0, LAST_CAST)
+        quantise_result(0, 128, 256)
+        nc.sync.dma_start(out=words_out[:, :HALF], in_=out_codes[:, :HALF].bitcast(I32))
+        quantise_result(1, 0, 256)
+        nc.sync.dma_start(out=words_out[:, HALF:], in_=out_codes[:, HALF:].bitcast(I32))
         for q in range(QUADS):
             queue = nc.sync if q % 2 == 0 else nc.scalar
             queue.dma_start(

@@ -23,8 +23,10 @@ QUADS = 4
 HALF = S // 2
 STORE_AFTER = ((1, 2, 4), (2, 4))
 LAST_CAST = 44
-VALUE_SHARES = ((128,), (152,), (152,), (172,))
-LAST_SPANS = ((0, 512),)
+GATE_SHARES = (((0, 0),), ((0, 0),), ((128, 0),), ((104, 0),))
+VALUE_SHARES = (((128, 24),), ((128, 24),), ((128, 0),), ((64, 0), (64, 24)))
+GELUS_AFTER = ((), ((0, (0, 1, 2, 3)),), (), ((1, (0, 1, 2, 3)),))
+LAST_SPANS = ((0, 256), (256, 512))
 
 
 def tile_picked_zmtp_gelu_po_kernel(
@@ -99,35 +101,30 @@ def tile_picked_zmtp_gelu_po_kernel(
             picked_scales[n] = sb("picked_scales_" + n, [P, S], U8, tag=tag)
             nc.vector.tensor_copy(out=picked_scales[n][:], in_=table_scales[n][:].indirect(lists[n][:]))
 
-        def quantise(name, g, on_vector, narrow=False):
+        def quantise(name, g, on_vector):
             rounded = [sb("rounded_%s%d_%d" % (name, g, u), [P, 2, P, PACK], BF16) for u in range(2)]
+            codes = [sb("codes_%s%d_%d" % (name, g, u), [P, 2 * P], U32) for u in range(2)]
+            scales = [sb("wscales_%s%d_%d" % (name, g, u), [P, 2 * P], U8) for u in range(2)]
             for (tile, c0, c1), share in zip(raw[name, g], on_vector):
+                m0, m1 = c0 // PACK, c1 // PACK
                 for u in range(2):
                     src = tile.rearrange("p j (m t) -> p m j t", t=PACK)[:, :, :, 2 * u : 2 * u + 2]
-                    dst = rounded[u][:, :, c0 // PACK : c1 // PACK, :].rearrange("p t m j -> p m j t")
-                    width = (c1 - c0) // PACK
-                    cut = min(max(share - u * width, 0), width)
+                    dst = rounded[u][:, :, m0:m1, :].rearrange("p t m j -> p m j t")
+                    cut = share[u]
                     if cut > 0:
                         nc.vector.tensor_copy(out=dst[:, :cut], in_=src[:, :cut])
-                    if cut < width:
+                    if cut < m1 - m0:
                         nc.scalar.copy(out=dst[:, cut:], in_=src[:, cut:])
-            operands = []
-            for u in range(2):
-                codes = sb("codes_%s%d_%d" % (name, g, u), [P, 2 * P], U32)
-                scales = sb("wscales_%s%d_%d" % (name, g, u), [P, 2 * P], U8)
-                flat = rounded[u][:].rearrange("p t m j -> p (t m j)")
-                if narrow:
-                    for v in range(2):
+                for u in range(2):
+                    flat = rounded[u][:].rearrange("p t m j -> p (t m j)")
+                    runs = ((0, 2 * P),) if m1 - m0 == P else ((m0, m1), (P + m0, P + m1))
+                    for r0, r1 in runs:
                         nc.vector.quantize_mx(
-                            out=codes[:, v * P : (v + 1) * P].bitcast(FP8X4),
-                            scales=scales[:, v * P : (v + 1) * P],
-                            in_=flat[:, v * K_PASS : (v + 1) * K_PASS],
+                            out=codes[u][:, r0:r1].bitcast(FP8X4),
+                            scales=scales[u][:, r0:r1],
+                            in_=flat[:, PACK * r0 : PACK * r1],
                         )
-                else:
-                    nc.vector.quantize_mx(out=codes[:].bitcast(FP8X4), scales=scales[:], in_=flat)
-                for v in range(2):
-                    operands.append((codes[:, v * P : (v + 1) * P], scales[:, v * P : (v + 1) * P]))
-            return operands
+            return [(codes[u][:, v * P : (v + 1) * P], scales[u][:, v * P : (v + 1) * P]) for u in range(2) for v in range(2)]
 
         def multiply(acc, operand, n, g, c0, c1, start, stop):
             plane = tables[n][3] + 4 * g
@@ -145,30 +142,31 @@ def tile_picked_zmtp_gelu_po_kernel(
         gate = {}
 
         def products(operands, side, n, g, start, stop):
-            for h in range(2):
-                for t in range(PACK):
-                    multiply(bank[h, t][:, side, :], operands[t], n, g, h * HALF, (h + 1) * HALF, start, stop)
+            order = [(h, t) for h in range(2) for t in range(PACK)]
+            if not stop:
+                order = sorted(order, key=lambda ht: ht[1] // 2)
+            for h, t in order:
+                multiply(bank[h, t][:, side, :], operands[t], n, g, h * HALF, (h + 1) * HALF, start, stop)
 
-        def gelu(h, slots, tag):
-            tile = sb("gate%d%d" % (h, slots[0]), [P, len(slots), HALF], F32, tag=tag)
-            for i, t in enumerate(slots):
+        def gelu(banks, tag):
+            if not banks:
+                return
+            tile = sb("gate%d%d" % banks[0], [P, len(banks), HALF], F32, tag=tag)
+            for i, (h, t) in enumerate(banks):
                 gate[h, t] = tile[:, i, :]
                 nc.scalar.activation(out=gate[h, t], in_=bank[h, t][:, 0, :], func=GELU)
 
         gate_pieces = (("w1", "x", 0), ("w1", "x", 1), ("w2", "e", 0), ("w2", "e", 1))
         for i, (name, n, g) in enumerate(gate_pieces):
             gather_words(n, g)
-            operands = quantise(name, g, (P * (i // 2),))
+            operands = quantise(name, g, GATE_SHARES[i])
             if g == 0:
                 gather_scales(n, ("rounded_w10_1", "rounded_w20_0")[i // 2])
             products(operands, 0, n, g, i == 0, i == 3)
         value_pieces = (("w3", "x", 0), ("w3", "x", 1), ("w4", "e", 0), ("w4", "e", 1))
         for i, (name, n, g) in enumerate(value_pieces):
-            operands = quantise(name, g, VALUE_SHARES[i], narrow=i == 3)
-            if i in (1, 2):
-                gelu(0, (2 * i - 2, 2 * i - 1), "raw_%s%d_0" % (name, g))
-            if i == 3:
-                gelu(1, (0, 1, 2, 3), "raw_w41_0")
+            operands = quantise(name, g, VALUE_SHARES[i])
+            gelu([(h, t) for h, slots in GELUS_AFTER[i] for t in slots], "raw_%s%d_%d" % (name, g, raw[name, g][-1][1]))
             products(operands, 1, n, g, i == 0, i == 3)
 
         out_rows = out_0.rearrange("(p t) c -> p t c", t=PACK)
@@ -190,24 +188,33 @@ def tile_picked_zmtp_gelu_po_kernel(
                 in_=sides[h][:, c0:c1, :].rearrange("p n t -> p (n t)"),
             )
 
-        for h in range(2):
-            cols = slice(h * HALF, (h + 1) * HALF)
-            stored = 0
-            for t in range(PACK):
-                nc.vector.tensor_tensor(out=results[h][:, t, :], in0=bank[h, t][:, 1, :], in1=gate[h, t], op=MULT)
-                if t + 1 in STORE_AFTER[h]:
-                    nc.sync.dma_start(out=out_rows[:, stored : t + 1, cols], in_=results[h][:, stored : t + 1, :])
-                    stored = t + 1
-            if h == 0:
-                cast(nc.scalar.copy, 0, 0, 32)
-                cast(nc.scalar.copy, 0, 32, 64)
-        cast(nc.scalar.copy, 1, LAST_CAST, 64)
-        quantise_result(0, 0, 128)
-        cast(nc.vector.tensor_copy, 1, 0, LAST_CAST)
-        quantise_result(0, 128, 256)
-        nc.sync.dma_start(out=words_out[:, :HALF], in_=out_codes[:, :HALF].bitcast(I32))
-        quantise_result(1, 0, 256)
-        nc.sync.dma_start(out=words_out[:, HALF:], in_=out_codes[:, HALF:].bitcast(I32))
+        def product(h, t, c0, c1):
+            nc.vector.tensor_tensor(
+                out=results[h][:, t, c0:c1], in0=bank[h, t][:, 1, c0:c1], in1=gate[h, t][:, c0:c1], op=MULT
+            )
+
+        def store(h, t0, t1):
+            nc.sync.dma_start(out=out_rows[:, t0:t1, h * HALF : (h + 1) * HALF], in_=results[h][:, t0:t1, :])
+
+        for t in range(PACK):
+            product(0, t, 0, HALF)
+            if t != 2:
+                store(0, min(t, 2), t + 1)
+        cast(nc.scalar.copy, 0, 0, 32)
+        cast(nc.scalar.copy, 0, 32, 64)
+        for t in range(PACK):
+            product(1, t, 0, P)
+        for t in range(PACK):
+            product(1, t, P, HALF)
+            if t % 2 == 1:
+                store(1, t - 1, t + 1)
+        cast(nc.scalar.copy, 1, 32, 64)
+        cast(nc.vector.tensor_copy, 1, 0, 32)
+        quantise_result(0, 0, HALF)
+        quantise_result(1, 0, P)
+        nc.sync.dma_start(out=words_out[:, : S - P], in_=out_codes[:, : S - P].bitcast(I32))
+        quantise_result(1, P, HALF)
+        nc.sync.dma_start(out=words_out[:, S - P :], in_=out_codes[:, S - P :].bitcast(I32))
         for q in range(QUADS):
             queue = nc.sync if q % 2 == 0 else nc.scalar
             queue.dma_start(

@@ -145,6 +145,8 @@ def tile_picked_zmtp_gelu_po_kernel(
             order = [(h, t) for h in range(2) for t in range(PACK)]
             if not stop:
                 order = sorted(order, key=lambda ht: ht[1] // 2)
+            elif side == 1:
+                order = order[:2] + order[4:5] + order[2:4] + order[5:]
             for h, t in order:
                 multiply(bank[h, t][:, side, :], operands[t], n, g, h * HALF, (h + 1) * HALF, start, stop)
 
@@ -200,16 +202,20 @@ def tile_picked_zmtp_gelu_po_kernel(
             product(0, t, 0, HALF)
             if t != 2:
                 store(0, min(t, 2), t + 1)
+        values = sb("values", [P, HALF], F32)
+        nc.scalar.copy(out=values[:], in_=bank[1, 0][:, 1, :])
+        nc.gpsimd.tensor_tensor(out=results[1][:, 0, :], in0=values[:], in1=gate[1, 0], op=MULT)
         cast(nc.scalar.copy, 0, 0, 32)
         cast(nc.scalar.copy, 0, 32, 64)
-        for t in range(PACK):
+        for t in range(1, PACK):
             product(1, t, 0, P)
-        for t in range(PACK):
+        for t in range(1, PACK):
             product(1, t, P, HALF)
             if t % 2 == 1:
                 store(1, t - 1, t + 1)
-        cast(nc.scalar.copy, 1, 32, 64)
+        cast(nc.scalar.copy, 1, 46, 64)
         cast(nc.vector.tensor_copy, 1, 0, 32)
+        cast(nc.vector.tensor_copy, 1, 32, 46)
         quantise_result(0, 0, HALF)
         quantise_result(1, 0, P)
         nc.sync.dma_start(out=words_out[:, : S - P], in_=out_codes[:, : S - P].bitcast(I32))

@@ -24,7 +24,7 @@ HALF = S // 2
 STORE_AFTER = ((1, 2, 4), (2, 4))
 LAST_CAST = 44
 GATE_SHARES = (((0, 0),), ((0, 0),), ((128, 0),), ((104, 0),))
-VALUE_SHARES = (((128, 24),), ((128, 24),), ((128, 0),), ((64, 0), (64, 24)))
+VALUE_SHARES = (((128, 24),), ((128, 24),), ((128, 0),), ((64, 0), (44, 44)))
 GELUS_AFTER = ((), ((0, (0, 1, 2, 3)),), (), ((1, (0, 1, 2, 3)),))
 LAST_SPANS = ((0, 256), (256, 512))
 
@@ -117,7 +117,7 @@ def tile_picked_zmtp_gelu_po_kernel(
                         nc.scalar.copy(out=dst[:, cut:], in_=src[:, cut:])
                 for u in range(2):
                     flat = rounded[u][:].rearrange("p t m j -> p (t m j)")
-                    runs = ((0, 2 * P),) if m1 - m0 == P else ((m0, m1), (P + m0, P + m1))
+                    runs = ((m0, m1), (P + m0, P + m1)) if (name, g) == ("w4", 1) else ((0, 2 * P),)
                     for r0, r1 in runs:
                         nc.vector.quantize_mx(
                             out=codes[u][:, r0:r1].bitcast(FP8X4),
@@ -207,12 +207,12 @@ def tile_picked_zmtp_gelu_po_kernel(
         nc.gpsimd.tensor_tensor(out=results[1][:, 0, :], in0=values[:], in1=gate[1, 0], op=MULT)
         cast(nc.scalar.copy, 0, 0, 32)
         cast(nc.scalar.copy, 0, 32, 64)
-        for t in range(1, PACK):
-            product(1, t, 0, P)
-        for t in range(1, PACK):
-            product(1, t, P, HALF)
-            if t % 2 == 1:
-                store(1, t - 1, t + 1)
+        product(1, 1, 0, HALF)
+        store(1, 0, 2)
+        for c0 in (0, P):
+            for t in range(2, PACK):
+                product(1, t, c0, c0 + P)
+        store(1, 2, PACK)
         cast(nc.scalar.copy, 1, 46, 64)
         cast(nc.vector.tensor_copy, 1, 0, 32)
         cast(nc.vector.tensor_copy, 1, 32, 46)

@@ -42,7 +42,7 @@ def tile_picked_zmtp_gelu_po_kernel(
 
         tables = {"x": (x_words, x_scales, offs, 0), "e": (e_words, e_scales, tok, 8)}
         lists = {name: keep.tile([P, S // 16], U16, name="list_" + name) for name in tables}
-        table_words = {n: sb("words_" + n, [P, PASSES, T], I32) for n in tables}
+        table_words = {}
         table_scales = {n: sb("scales_" + n, [P, T], U8) for n in tables}
         picked_words = {(n, g): sb("picked_words_%s%d" % (n, g), [P, S], U32) for n in tables for g in range(PASSES)}
         picked_scales = {}
@@ -61,12 +61,15 @@ def tile_picked_zmtp_gelu_po_kernel(
                     in_=tables[n][1][:, 4 * q : 4 * q + 4, :].bitcast(I32),
                 )
 
-        def load_table(n):
-            nc.sync.dma_start(
-                out=table_words[n][:],
-                in_=tables[n][0].rearrange("g p n t -> p g (n t)").bitcast(I32),
-            )
-            nc.sync.dma_start(lists[n][:], tables[n][2])
+        def load_table(n, spans):
+            words = tables[n][0].rearrange("g p n t -> p g (n t)").bitcast(I32)
+            for g0, g1 in spans:
+                tile = sb("words_%s%d" % (n, g0), [P, g1 - g0, T], I32)
+                nc.sync.dma_start(out=tile[:], in_=words[:, g0:g1, :])
+                if g0 == 0:
+                    nc.sync.dma_start(lists[n][:], tables[n][2])
+                for g in range(g0, g1):
+                    table_words[n, g] = tile[:, g - g0, :]
 
         raw = {}
 
@@ -80,10 +83,10 @@ def tile_picked_zmtp_gelu_po_kernel(
 
         load_scales("x")
         load_scales("e")
-        load_table("x")
+        load_table("x", ((0, 2),))
         load_pass("w1", w1, 0, ((0, N),))
         load_pass("w1", w1, 1, ((0, N),))
-        load_table("e")
+        load_table("e", ((0, 1), (1, 2)))
         load_pass("w2", w2, 0, ((0, N),))
         load_pass("w2", w2, 1, ((0, N),))
         load_pass("w3", w3, 0, ((0, N),))
@@ -94,7 +97,7 @@ def tile_picked_zmtp_gelu_po_kernel(
         def gather_words(n, g):
             nc.vector.tensor_copy(
                 out=picked_words[n, g][:],
-                in_=table_words[n][:, g, :].bitcast(U32).indirect(lists[n][:]),
+                in_=table_words[n, g].bitcast(U32).indirect(lists[n][:]),
             )
 
         def gather_scales(n, tag):
@@ -200,8 +203,8 @@ def tile_picked_zmtp_gelu_po_kernel(
 
         for t in range(PACK):
             product(0, t, 0, HALF)
-            if t != 2:
-                store(0, min(t, 2), t + 1)
+            if t % 2 == 1:
+                store(0, t - 1, t + 1)
         values = sb("values", [P, HALF], F32)
         nc.scalar.copy(out=values[:], in_=bank[1, 0][:, 1, :])
         nc.gpsimd.tensor_tensor(out=results[1][:, 0, :], in0=values[:], in1=gate[1, 0], op=MULT)
@@ -216,11 +219,10 @@ def tile_picked_zmtp_gelu_po_kernel(
         cast(nc.scalar.copy, 1, 46, 64)
         cast(nc.vector.tensor_copy, 1, 0, 32)
         cast(nc.vector.tensor_copy, 1, 32, 46)
-        quantise_result(0, 0, HALF)
-        quantise_result(1, 0, P)
-        nc.sync.dma_start(out=words_out[:, : S - P], in_=out_codes[:, : S - P].bitcast(I32))
-        quantise_result(1, P, HALF)
-        nc.sync.dma_start(out=words_out[:, S - P :], in_=out_codes[:, S - P :].bitcast(I32))
+        for h in range(2):
+            quantise_result(h, 0, HALF)
+            cols = slice(h * HALF, (h + 1) * HALF)
+            nc.sync.dma_start(out=words_out[:, cols], in_=out_codes[:, cols].bitcast(I32))
         for q in range(QUADS):
             queue = nc.sync if q % 2 == 0 else nc.scalar
             queue.dma_start(

@@ -21,12 +21,7 @@ K_PASS = P * PACK
 PASSES = K // K_PASS
 QUADS = 4
 HALF = S // 2
-STORE_AFTER = ((1, 2, 4), (2, 4))
-LAST_CAST = 44
-GATE_SHARES = (((0, 0),), ((0, 0),), ((128, 0),), ((104, 0),))
-VALUE_SHARES = (((128, 24),), ((128, 24),), ((128, 0),), ((64, 0), (44, 44)))
-GELUS_AFTER = ((), ((0, (0, 1, 2, 3)),), (), ((1, (0, 1, 2, 3)),))
-LAST_SPANS = ((0, 256), (256, 512))
+CHUNK = S // 4
 
 
 def tile_picked_zmtp_gelu_po_kernel(
@@ -73,26 +68,26 @@ def tile_picked_zmtp_gelu_po_kernel(
 
         raw = {}
 
-        def load_pass(name, w, g, spans):
+        def load_pass(name, w, g, c0, c1):
             rows = w[g * K_PASS : (g + 1) * K_PASS, :].rearrange("(p j) c -> p j c", j=PACK)
-            raw[name, g] = []
-            for c0, c1 in spans:
-                tile = sb("raw_%s%d_%d" % (name, g, c0), [P, PACK, c1 - c0], F32)
-                nc.sync.dma_start(out=tile[:], in_=rows[:, :, c0:c1])
-                raw[name, g].append((tile[:], c0, c1))
+            tile = sb("raw_%s%d_%d" % (name, g, c0), [P, PACK, c1 - c0], F32)
+            nc.sync.dma_start(out=tile[:], in_=rows[:, :, c0:c1])
+            raw[name, g, c0] = tile[:]
 
         load_scales("x")
         load_scales("e")
         load_table("x", ((0, 2),))
-        load_pass("w1", w1, 0, ((0, N),))
-        load_pass("w1", w1, 1, ((0, N),))
+        for g in range(PASSES):
+            load_pass("w1", w1, g, 0, N)
         load_table("e", ((0, 1), (1, 2)))
-        load_pass("w2", w2, 0, ((0, N),))
-        load_pass("w2", w2, 1, ((0, N),))
-        load_pass("w3", w3, 0, ((0, N),))
-        load_pass("w3", w3, 1, ((0, N),))
-        load_pass("w4", w4, 0, ((0, N),))
-        load_pass("w4", w4, 1, LAST_SPANS)
+        for name, w in (("w2", w2), ("w3", w3)):
+            for g in range(PASSES):
+                load_pass(name, w, g, 0, N)
+        load_pass("w4", w4, 0, 0, N)
+        last_rows = w4[K_PASS:K, :].rearrange("(p j) c -> p j c", j=PACK)
+        for d in range(2):
+            raw["last", d] = sb("raw_last%d" % d, [P, 2, N], F32)
+            nc.sync.dma_start(out=raw["last", d][:], in_=last_rows[:, 2 * d : 2 * d + 2, :])
 
         def gather_words(n, g):
             nc.vector.tensor_copy(
@@ -104,127 +99,177 @@ def tile_picked_zmtp_gelu_po_kernel(
             picked_scales[n] = sb("picked_scales_" + n, [P, S], U8, tag=tag)
             nc.vector.tensor_copy(out=picked_scales[n][:], in_=table_scales[n][:].indirect(lists[n][:]))
 
-        def quantise(name, g, on_vector):
-            rounded = [sb("rounded_%s%d_%d" % (name, g, u), [P, 2, P, PACK], BF16) for u in range(2)]
-            codes = [sb("codes_%s%d_%d" % (name, g, u), [P, 2 * P], U32) for u in range(2)]
-            scales = [sb("wscales_%s%d_%d" % (name, g, u), [P, 2 * P], U8) for u in range(2)]
-            for (tile, c0, c1), share in zip(raw[name, g], on_vector):
-                m0, m1 = c0 // PACK, c1 // PACK
-                for u in range(2):
-                    src = tile.rearrange("p j (m t) -> p m j t", t=PACK)[:, :, :, 2 * u : 2 * u + 2]
-                    dst = rounded[u][:, :, m0:m1, :].rearrange("p t m j -> p m j t")
-                    cut = share[u]
-                    if cut > 0:
-                        nc.vector.tensor_copy(out=dst[:, :cut], in_=src[:, :cut])
-                    if cut < m1 - m0:
-                        nc.scalar.copy(out=dst[:, cut:], in_=src[:, cut:])
-                for u in range(2):
-                    flat = rounded[u][:].rearrange("p t m j -> p (t m j)")
-                    runs = ((m0, m1), (P + m0, P + m1)) if (name, g) == ("w4", 1) else ((0, 2 * P),)
-                    for r0, r1 in runs:
-                        nc.vector.quantize_mx(
-                            out=codes[u][:, r0:r1].bitcast(FP8X4),
-                            scales=scales[u][:, r0:r1],
-                            in_=flat[:, PACK * r0 : PACK * r1],
-                        )
-            return [(codes[u][:, v * P : (v + 1) * P], scales[u][:, v * P : (v + 1) * P]) for u in range(2) for v in range(2)]
+        rounded, codes, wscales = {}, {}, {}
 
-        def multiply(acc, operand, n, g, c0, c1, start, stop):
-            plane = tables[n][3] + 4 * g
-            nc.tensor.matmul_mx(
-                out=acc,
-                lhsT=operand[0].bitcast(FP8X4),
-                lhsT_scale=operand[1],
-                rhs=picked_words[n, g][:, c0:c1].bitcast(FP8X4),
-                rhs_scale=picked_scales[n][plane:, c0:c1],
-                start=start,
-                stop=stop,
+        def round_columns(name, g, c0, c1, on_vector):
+            if c0 == 0:
+                for u in range(2):
+                    rounded[name, g, u] = sb("rounded_%s%d_%d" % (name, g, u), [P, 2, P, PACK], BF16)
+                    codes[name, g, u] = sb("codes_%s%d_%d" % (name, g, u), [P, 2 * P], U32)
+                    wscales[name, g, u] = sb("wscales_%s%d_%d" % (name, g, u), [P, 2 * P], U8)
+            m0, m1 = c0 // PACK, c1 // PACK
+            for u in range(2):
+                src = raw[name, g, c0].rearrange("p j (m t) -> p m j t", t=PACK)[:, :, :, 2 * u : 2 * u + 2]
+                dst = rounded[name, g, u][:, :, m0:m1, :].rearrange("p t m j -> p m j t")
+                cut = on_vector[u]
+                if cut > 0:
+                    nc.vector.tensor_copy(out=dst[:, :cut], in_=src[:, :cut])
+                if cut < m1 - m0:
+                    nc.scalar.copy(out=dst[:, cut:], in_=src[:, cut:])
+
+        def quantise_words(name, g, u, r0, r1):
+            flat = rounded[name, g, u][:].rearrange("p t m j -> p (t m j)")
+            nc.vector.quantize_mx(
+                out=codes[name, g, u][:, r0:r1].bitcast(FP8X4),
+                scales=wscales[name, g, u][:, r0:r1],
+                in_=flat[:, PACK * r0 : PACK * r1],
             )
 
-        bank = {(h, t): psum.tile([P, 2, HALF], F32, name="bank%d%d" % (h, t)) for h in range(2) for t in range(PACK)}
+        def quantise(name, g, on_vector):
+            round_columns(name, g, 0, N, on_vector)
+            for u in range(2):
+                quantise_words(name, g, u, 0, 2 * P)
+
+        sums = {}
+        paired = {}
+        for h, t in [(0, 0), (0, 1), (0, 2), (0, 3), (1, 0), (1, 1)]:
+            bank = psum.tile([P, 2, HALF], F32, name="bank%d%d" % (h, t))
+            for side in range(2):
+                sums[h, t, side] = bank[:, side, :]
+        for side in range(2):
+            paired[1, side] = psum.tile([P, 2, HALF], F32, name="paired%d" % side)
+            for t in (2, 3):
+                sums[1, t, side] = paired[1, side][:, t - 2, :]
+
+        def multiply(name, n, g, side, order, start, stop):
+            plane = tables[n][3] + 4 * g
+            for h, t in order:
+                cols = slice((t % 2) * P, (t % 2 + 1) * P)
+                nc.tensor.matmul_mx(
+                    out=sums[h, t, side],
+                    lhsT=codes[name, g, t // 2][:, cols].bitcast(FP8X4),
+                    lhsT_scale=wscales[name, g, t // 2][:, cols],
+                    rhs=picked_words[n, g][:, h * HALF : (h + 1) * HALF].bitcast(FP8X4),
+                    rhs_scale=picked_scales[n][plane:, h * HALF : (h + 1) * HALF],
+                    start=start and (h, t) != (1, 3),
+                    stop=stop and (h, t) != (1, 2),
+                )
+
+        by_slot = [(h, t) for u in range(2) for h in range(2) for t in (2 * u, 2 * u + 1)]
         gate = {}
 
-        def products(operands, side, n, g, start, stop):
-            order = [(h, t) for h in range(2) for t in range(PACK)]
-            if not stop:
-                order = sorted(order, key=lambda ht: ht[1] // 2)
-            elif side == 1:
-                order = order[:2] + order[4:5] + order[2:4] + order[5:]
-            for h, t in order:
-                multiply(bank[h, t][:, side, :], operands[t], n, g, h * HALF, (h + 1) * HALF, start, stop)
+        def gelu(h, u, tag):
+            gate[h, u] = sb("gate%d%d" % (h, u), [P, 2, HALF], F32, tag=tag)
+            if (h, u) == (1, 1):
+                nc.scalar.activation(out=gate[h, u][:], in_=paired[h, 0][:], func=GELU)
+            else:
+                for t in range(2):
+                    nc.scalar.activation(out=gate[h, u][:, t, :], in_=sums[h, 2 * u + t, 0], func=GELU)
 
-        def gelu(banks, tag):
-            if not banks:
-                return
-            tile = sb("gate%d%d" % banks[0], [P, len(banks), HALF], F32, tag=tag)
-            for i, (h, t) in enumerate(banks):
-                gate[h, t] = tile[:, i, :]
-                nc.scalar.activation(out=gate[h, t], in_=bank[h, t][:, 0, :], func=GELU)
-
-        gate_pieces = (("w1", "x", 0), ("w1", "x", 1), ("w2", "e", 0), ("w2", "e", 1))
-        for i, (name, n, g) in enumerate(gate_pieces):
-            gather_words(n, g)
-            operands = quantise(name, g, GATE_SHARES[i])
-            if g == 0:
-                gather_scales(n, ("rounded_w10_1", "rounded_w20_0")[i // 2])
-            products(operands, 0, n, g, i == 0, i == 3)
-        value_pieces = (("w3", "x", 0), ("w3", "x", 1), ("w4", "e", 0), ("w4", "e", 1))
-        for i, (name, n, g) in enumerate(value_pieces):
-            operands = quantise(name, g, VALUE_SHARES[i])
-            gelu([(h, t) for h, slots in GELUS_AFTER[i] for t in slots], "raw_%s%d_%d" % (name, g, raw[name, g][-1][1]))
-            products(operands, 1, n, g, i == 0, i == 3)
+        by_half = sorted(by_slot)
+        gather_words("x", 0)
+        quantise("w1", 0, (0, 0))
+        gather_scales("x", "rounded_w10_1")
+        multiply("w1", "x", 0, 0, by_slot, True, False)
+        gather_words("x", 1)
+        quantise("w1", 1, (0, 0))
+        multiply("w1", "x", 1, 0, by_slot, False, False)
+        gather_words("e", 0)
+        quantise("w2", 0, (128, 0))
+        gather_scales("e", "rounded_w20_0")
+        multiply("w2", "e", 0, 0, by_slot, False, False)
+        gather_words("e", 1)
+        quantise("w2", 1, (104, 0))
+        multiply("w2", "e", 1, 0, by_half, False, True)
+        quantise("w3", 0, (128, 24))
+        gelu(0, 0, "raw_w30_0")
+        multiply("w3", "x", 0, 1, by_slot[2:] + by_slot[:2], True, False)
+        quantise("w3", 1, (128, 24))
+        gelu(0, 1, "raw_w31_0")
+        gelu(1, 0, "rounded_w31_0")
+        multiply("w3", "x", 1, 1, by_slot, False, False)
+        quantise("w4", 0, (128, 48))
+        multiply("w4", "e", 0, 1, by_slot, False, False)
+        for u in range(2):
+            rounded["w4", 1, u] = sb("rounded_w41_%d" % u, [P, 2, P, PACK], BF16)
+            codes["w4", 1, u] = sb("codes_w41_%d" % u, [P, 2 * P], U32)
+            wscales["w4", 1, u] = sb("wscales_w41_%d" % u, [P, 2 * P], U8)
+        for d, on_vector in enumerate(((128, 0), (88, 64))):
+            for u in range(2):
+                src = raw["last", d][:].rearrange("p j (m t) -> p m j t", t=PACK)[:, :, :, 2 * u : 2 * u + 2]
+                dst = rounded["w4", 1, u][:, :, :, 2 * d : 2 * d + 2].rearrange("p t m j -> p m j t")
+                cut = on_vector[u]
+                if cut > 0:
+                    nc.vector.tensor_copy(out=dst[:, :cut], in_=src[:, :cut])
+                if cut < P:
+                    nc.scalar.copy(out=dst[:, cut:], in_=src[:, cut:])
+        for r0 in (0, P):
+            quantise_words("w4", 1, 0, r0, r0 + P)
+        quantise_words("w4", 1, 1, 0, 2 * P)
+        gelu(1, 1, "raw_last1")
+        last = [(0, 0), (0, 1), (1, 0), (0, 2), (0, 3), (1, 1), (1, 2), (1, 3)]
+        multiply("w4", "e", 1, 1, last, False, True)
 
         out_rows = out_0.rearrange("(p t) c -> p t c", t=PACK)
         out_codes = sb("out_codes", [P, S], U32)
         out_scales = sb("out_scales", [P, S], U8)
-        words_out = out_1[0].rearrange("p n t -> p (n t)").bitcast(I32)
         results = [sb("result%d" % h, [P, PACK, HALF], F32) for h in range(2)]
         sides = [sb("side%d" % h, [P, HALF, PACK], BF16) for h in range(2)]
 
-        def cast(engine_copy, h, a0, a1):
-            src = results[h][:].rearrange("p t (a i) -> p a t i", i=4)
-            dst = sides[h][:].rearrange("p (a i) t -> p a t i", i=4)
-            engine_copy(out=dst[:, a0:a1], in_=src[:, a0:a1])
+        def product(h, t):
+            nc.vector.tensor_tensor(out=results[h][:, t, :], in0=sums[h, t, 1], in1=gate[h, 0][:, t, :], op=MULT)
 
-        def quantise_result(h, c0, c1):
-            nc.vector.quantize_mx(
-                out=out_codes[:, h * HALF + c0 : h * HALF + c1].bitcast(FP8X4),
-                scales=out_scales[:, h * HALF + c0 : h * HALF + c1],
-                in_=sides[h][:, c0:c1, :].rearrange("p n t -> p (n t)"),
-            )
-
-        def product(h, t, c0, c1):
+        def paired_product(h, c0, c1):
             nc.vector.tensor_tensor(
-                out=results[h][:, t, c0:c1], in0=bank[h, t][:, 1, c0:c1], in1=gate[h, t][:, c0:c1], op=MULT
+                out=results[h][:, 2:PACK, c0:c1], in0=paired[h, 1][:, :, c0:c1], in1=gate[h, 1][:, :, c0:c1], op=MULT
             )
 
         def store(h, t0, t1):
             nc.sync.dma_start(out=out_rows[:, t0:t1, h * HALF : (h + 1) * HALF], in_=results[h][:, t0:t1, :])
 
-        for t in range(PACK):
-            product(0, t, 0, HALF)
-            if t % 2 == 1:
-                store(0, t - 1, t + 1)
+        def cast(engine_copy, h, c0, c1):
+            src = results[h][:, :, c0:c1].rearrange("p t (a i) -> p a t i", i=4)
+            dst = sides[h][:, c0:c1, :].rearrange("p (a i) t -> p a t i", i=4)
+            engine_copy(out=dst, in_=src)
+
+        def quantise_result(h):
+            nc.vector.quantize_mx(
+                out=out_codes[:, h * HALF : (h + 1) * HALF].bitcast(FP8X4),
+                scales=out_scales[:, h * HALF : (h + 1) * HALF],
+                in_=sides[h][:].rearrange("p n t -> p (n t)"),
+            )
+
         values = sb("values", [P, HALF], F32)
-        nc.scalar.copy(out=values[:], in_=bank[1, 0][:, 1, :])
-        nc.gpsimd.tensor_tensor(out=results[1][:, 0, :], in0=values[:], in1=gate[1, 0], op=MULT)
-        cast(nc.scalar.copy, 0, 0, 32)
-        cast(nc.scalar.copy, 0, 32, 64)
-        product(1, 1, 0, HALF)
+        product(0, 0)
+        product(0, 1)
+        store(0, 0, 2)
+        nc.scalar.copy(out=values[:], in_=sums[1, 0, 1])
+        nc.gpsimd.tensor_tensor(out=results[1][:, 0, :], in0=values[:], in1=gate[1, 0][:, 0, :], op=MULT)
+        for c0 in (0, CHUNK):
+            for t in (2, 3):
+                nc.vector.tensor_tensor(
+                    out=results[0][:, t, c0 : c0 + CHUNK],
+                    in0=sums[0, t, 1][:, c0 : c0 + CHUNK],
+                    in1=gate[0, 1][:, t - 2, c0 : c0 + CHUNK],
+                    op=MULT,
+                )
+            cast(nc.scalar.copy, 0, c0, c0 + CHUNK)
+        store(0, 2, PACK)
+        product(1, 1)
         store(1, 0, 2)
-        for c0 in (0, P):
-            for t in range(2, PACK):
-                product(1, t, c0, c0 + P)
+        for c0 in (0, CHUNK):
+            paired_product(1, c0, c0 + CHUNK)
         store(1, 2, PACK)
-        cast(nc.scalar.copy, 1, 46, 64)
-        cast(nc.vector.tensor_copy, 1, 0, 32)
-        cast(nc.vector.tensor_copy, 1, 32, 46)
+        cast(nc.scalar.copy, 1, 144, HALF)
+        cast(nc.vector.tensor_copy, 1, 0, CHUNK)
+        cast(nc.vector.tensor_copy, 1, CHUNK, 144)
+        words_out = out_1[0].rearrange("p n t -> p (n t)").bitcast(I32)
         for h in range(2):
-            quantise_result(h, 0, HALF)
+            quantise_result(h)
             cols = slice(h * HALF, (h + 1) * HALF)
-            nc.sync.dma_start(out=words_out[:, cols], in_=out_codes[:, cols].bitcast(I32))
+            nc.scalar.dma_start(out=words_out[:, cols], in_=out_codes[:, cols].bitcast(I32))
         for q in range(QUADS):
-            queue = nc.sync if q % 2 == 0 else nc.scalar
+            queue = nc.sync if q < QUADS - 1 else nc.scalar
             queue.dma_start(
                 out=out_2[0, 4 * q : 4 * q + 4, :].bitcast(I32),
                 in_=out_scales[32 * q : 32 * q + 4, :].bitcast(I32),

from contextlib import ExitStack

import concourse.mybir as mybir

K, T, S, N = 1024, 1024, 512, 512
FLOPS = 2 * 4 * K * N * S

F32 = mybir.dt.float32
BF16 = mybir.dt.bfloat16
I32 = mybir.dt.int32
U32 = mybir.dt.uint32
U16 = mybir.dt.uint16
U8 = mybir.dt.uint8
FP8X4 = mybir.dt.float8_e4m3fn_x4
GELU = mybir.ActivationFunctionType.Gelu_apprx_tanh
MULT = mybir.AluOpType.mult

P = 128
PACK = 4
K_PASS = P * PACK
PASSES = K // K_PASS
QUADS = 4
HALF = S // 2
CHUNK = S // 4


def tile_picked_zmtp_gelu_po_kernel(
    tc, x_words, x_scales, e_words, e_scales, w1, w2, w3, w4, offs, tok, out_0, out_1, out_2
):
    nc = tc.nc
    with ExitStack() as ctx:
        keep = ctx.enter_context(tc.tile_pool(name="keep", bufs=1))
        psum = ctx.enter_context(tc.psum_pool(name="psum", bufs=1))

        def sb(name, shape, dtype, tag=""):
            return keep.tile(shape, dtype, name=name, tag=tag or name, align_bytes=64)

        tables = {"x": (x_words, x_scales, offs, 0), "e": (e_words, e_scales, tok, 8)}
        lists = {name: keep.tile([P, S // 16], U16, name="list_" + name) for name in tables}
        table_words = {}
        table_scales = {n: sb("scales_" + n, [P, T], U8) for n in tables}
        picked_words = {(n, g): sb("picked_words_%s%d" % (n, g), [P, S], U32) for n in tables for g in range(PASSES)}
        picked_scales = {}

        nc.gpsimd.memset(table_scales["x"][:].bitcast(I32), 0)
        nc.vector.memset(table_scales["e"][:].bitcast(I32), 0)
        warm = sb("warm", [P, 2], F32)
        nc.vector.memset(warm[:, 0:1], 0.0)
        nc.scalar.activation(out=warm[:, 1:2], in_=warm[:, 0:1], func=GELU)

        def load_scales(n):
            for q in range(QUADS):
                row = 32 * q + tables[n][3]
                nc.gpsimd.dma_start(
                    out=table_scales[n][row : row + 4 * PASSES, :].bitcast(I32),
                    in_=tables[n][1][:, 4 * q : 4 * q + 4, :].bitcast(I32),
                )

        def load_table(n, spans):
            words = tables[n][0].rearrange("g p n t -> p g (n t)").bitcast(I32)
            for g0, g1 in spans:
                tile = sb("words_%s%d" % (n, g0), [P, g1 - g0, T], I32)
                nc.sync.dma_start(out=tile[:], in_=words[:, g0:g1, :])
                if g0 == 0:
                    nc.sync.dma_start(lists[n][:], tables[n][2])
                for g in range(g0, g1):
                    table_words[n, g] = tile[:, g - g0, :]

        raw = {}

        def load_pass(name, w, g, c0, c1):
            rows = w[g * K_PASS : (g + 1) * K_PASS, :].rearrange("(p j) c -> p j c", j=PACK)
            tile = sb("raw_%s%d_%d" % (name, g, c0), [P, PACK, c1 - c0], F32)
            nc.sync.dma_start(out=tile[:], in_=rows[:, :, c0:c1])
            raw[name, g, c0] = tile[:]

        load_scales("x")
        load_scales("e")
        load_table("x", ((0, 2),))
        for g in range(PASSES):
            load_pass("w1", w1, g, 0, N)
        load_table("e", ((0, 1), (1, 2)))
        for name, w in (("w2", w2), ("w3", w3)):
            for g in range(PASSES):
                load_pass(name, w, g, 0, N)
        load_pass("w4", w4, 0, 0, N)
        last_rows = w4[K_PASS:K, :].rearrange("(p j) c -> p j c", j=PACK)
        for d in range(2):
            raw["last", d] = sb("raw_last%d" % d, [P, 2, N], F32)
            nc.sync.dma_start(out=raw["last", d][:], in_=last_rows[:, 2 * d : 2 * d + 2, :])

        def gather_words(n, g):
            nc.vector.tensor_copy(
                out=picked_words[n, g][:],
                in_=table_words[n, g].bitcast(U32).indirect(lists[n][:]),
            )

        def gather_scales(n, tag):
            picked_scales[n] = sb("picked_scales_" + n, [P, S], U8, tag=tag)
            nc.vector.tensor_copy(out=picked_scales[n][:], in_=table_scales[n][:].indirect(lists[n][:]))

        rounded, codes, wscales = {}, {}, {}

        def round_columns(name, g, c0, c1, on_vector):
            if c0 == 0:
                for u in range(2):
                    rounded[name, g, u] = sb("rounded_%s%d_%d" % (name, g, u), [P, 2, P, PACK], BF16)
                    codes[name, g, u] = sb("codes_%s%d_%d" % (name, g, u), [P, 2 * P], U32)
                    wscales[name, g, u] = sb("wscales_%s%d_%d" % (name, g, u), [P, 2 * P], U8)
            m0, m1 = c0 // PACK, c1 // PACK
            for u in range(2):
                src = raw[name, g, c0].rearrange("p j (m t) -> p m j t", t=PACK)[:, :, :, 2 * u : 2 * u + 2]
                dst = rounded[name, g, u][:, :, m0:m1, :].rearrange("p t m j -> p m j t")
                cut = on_vector[u]
                if cut > 0:
                    nc.vector.tensor_copy(out=dst[:, :cut], in_=src[:, :cut])
                if cut < m1 - m0:
                    nc.scalar.copy(out=dst[:, cut:], in_=src[:, cut:])

        def quantise_words(name, g, u, r0, r1):
            flat = rounded[name, g, u][:].rearrange("p t m j -> p (t m j)")
            nc.vector.quantize_mx(
                out=codes[name, g, u][:, r0:r1].bitcast(FP8X4),
                scales=wscales[name, g, u][:, r0:r1],
                in_=flat[:, PACK * r0 : PACK * r1],
            )

        def quantise(name, g, on_vector):
            round_columns(name, g, 0, N, on_vector)
            for u in range(2):
                quantise_words(name, g, u, 0, 2 * P)

        sums = {}
        paired = {}
        for h, t in [(0, 0), (0, 1), (0, 2), (0, 3), (1, 0), (1, 1)]:
            bank = psum.tile([P, 2, HALF], F32, name="bank%d%d" % (h, t))
            for side in range(2):
                sums[h, t, side] = bank[:, side, :]
        for side in range(2):
            paired[1, side] = psum.tile([P, 2, HALF], F32, name="paired%d" % side)
            for t in (2, 3):
                sums[1, t, side] = paired[1, side][:, t - 2, :]

        def multiply(name, n, g, side, order, start, stop):
            plane = tables[n][3] + 4 * g
            for h, t in order:
                cols = slice((t % 2) * P, (t % 2 + 1) * P)
                nc.tensor.matmul_mx(
                    out=sums[h, t, side],
                    lhsT=codes[name, g, t // 2][:, cols].bitcast(FP8X4),
                    lhsT_scale=wscales[name, g, t // 2][:, cols],
                    rhs=picked_words[n, g][:, h * HALF : (h + 1) * HALF].bitcast(FP8X4),
                    rhs_scale=picked_scales[n][plane:, h * HALF : (h + 1) * HALF],
                    start=start and (h, t) != (1, 3),
                    stop=stop and (h, t) != (1, 2),
                )

        by_slot = [(h, t) for u in range(2) for h in range(2) for t in (2 * u, 2 * u + 1)]
        gate = {}

        def gelu(h, u, tag):
            gate[h, u] = sb("gate%d%d" % (h, u), [P, 2, HALF], F32, tag=tag)
            if (h, u) == (1, 1):
                nc.scalar.activation(out=gate[h, u][:], in_=paired[h, 0][:], func=GELU)
            else:
                for t in range(2):
                    nc.scalar.activation(out=gate[h, u][:, t, :], in_=sums[h, 2 * u + t, 0], func=GELU)

        by_half = sorted(by_slot)
        gather_words("x", 0)
        quantise("w1", 0, (0, 0))
        gather_scales("x", "rounded_w10_1")
        multiply("w1", "x", 0, 0, by_slot, True, False)
        gather_words("x", 1)
        quantise("w1", 1, (0, 0))
        multiply("w1", "x", 1, 0, by_slot, False, False)
        gather_words("e", 0)
        quantise("w2", 0, (128, 0))
        gather_scales("e", "rounded_w20_0")
        multiply("w2", "e", 0, 0, by_slot, False, False)
        gather_words("e", 1)
        quantise("w2", 1, (104, 0))
        multiply("w2", "e", 1, 0, by_half, False, True)
        quantise("w3", 0, (128, 24))
        gelu(0, 0, "raw_w30_0")
        multiply("w3", "x", 0, 1, by_slot[2:] + by_slot[:2], True, False)
        quantise("w3", 1, (128, 24))
        gelu(0, 1, "raw_w31_0")
        gelu(1, 0, "rounded_w31_0")
        multiply("w3", "x", 1, 1, by_slot, False, False)
        quantise("w4", 0, (128, 48))
        multiply("w4", "e", 0, 1, by_slot, False, False)
        for u in range(2):
            rounded["w4", 1, u] = sb("rounded_w41_%d" % u, [P, 2, P, PACK], BF16)
            codes["w4", 1, u] = sb("codes_w41_%d" % u, [P, 2 * P], U32)
            wscales["w4", 1, u] = sb("wscales_w41_%d" % u, [P, 2 * P], U8)
        for d, on_vector in enumerate(((128, 0), (88, 64))):
            for u in range(2):
                src = raw["last", d][:].rearrange("p j (m t) -> p m j t", t=PACK)[:, :, :, 2 * u : 2 * u + 2]
                dst = rounded["w4", 1, u][:, :, :, 2 * d : 2 * d + 2].rearrange("p t m j -> p m j t")
                cut = on_vector[u]
                if cut > 0:
                    nc.vector.tensor_copy(out=dst[:, :cut], in_=src[:, :cut])
                if cut < P:
                    nc.scalar.copy(out=dst[:, cut:], in_=src[:, cut:])
        for r0 in (0, P):
            quantise_words("w4", 1, 0, r0, r0 + P)
        quantise_words("w4", 1, 1, 0, 2 * P)
        gelu(1, 1, "raw_last1")
        last = [(0, 0), (0, 1), (1, 0), (0, 2), (0, 3), (1, 1), (1, 2), (1, 3)]
        multiply("w4", "e", 1, 1, last, False, True)

        out_rows = out_0.rearrange("(p t) c -> p t c", t=PACK)
        out_codes = sb("out_codes", [P, S], U32)
        out_scales = sb("out_scales", [P, S], U8)
        results = [sb("result%d" % h, [P, PACK, HALF], F32) for h in range(2)]
        sides = [sb("side%d" % h, [P, HALF, PACK], BF16) for h in range(2)]

        def product(h, t):
            nc.vector.tensor_tensor(out=results[h][:, t, :], in0=sums[h, t, 1], in1=gate[h, 0][:, t, :], op=MULT)

        def paired_product(h, c0, c1):
            nc.vector.tensor_tensor(
                out=results[h][:, 2:PACK, c0:c1], in0=paired[h, 1][:, :, c0:c1], in1=gate[h, 1][:, :, c0:c1], op=MULT
            )

        def store(h, t0, t1):
            nc.sync.dma_start(out=out_rows[:, t0:t1, h * HALF : (h + 1) * HALF], in_=results[h][:, t0:t1, :])

        def cast(engine_copy, h, c0, c1):
            src = results[h][:, :, c0:c1].rearrange("p t (a i) -> p a t i", i=4)
            dst = sides[h][:, c0:c1, :].rearrange("p (a i) t -> p a t i", i=4)
            engine_copy(out=dst, in_=src)

        def quantise_result(h):
            nc.vector.quantize_mx(
                out=out_codes[:, h * HALF : (h + 1) * HALF].bitcast(FP8X4),
                scales=out_scales[:, h * HALF : (h + 1) * HALF],
                in_=sides[h][:].rearrange("p n t -> p (n t)"),
            )

        values = sb("values", [P, HALF], F32)
        product(0, 0)
        product(0, 1)
        store(0, 0, 2)
        nc.scalar.copy(out=values[:], in_=sums[1, 0, 1])
        nc.gpsimd.tensor_tensor(out=results[1][:, 0, :], in0=values[:], in1=gate[1, 0][:, 0, :], op=MULT)
        for c0 in (0, CHUNK):
            for t in (2, 3):
                nc.vector.tensor_tensor(
                    out=results[0][:, t, c0 : c0 + CHUNK],
                    in0=sums[0, t, 1][:, c0 : c0 + CHUNK],
                    in1=gate[0, 1][:, t - 2, c0 : c0 + CHUNK],
                    op=MULT,
                )
            cast(nc.scalar.copy, 0, c0, c0 + CHUNK)
        store(0, 2, PACK)
        product(1, 1)
        store(1, 0, 2)
        for c0 in (0, CHUNK):
            paired_product(1, c0, c0 + CHUNK)
        store(1, 2, PACK)
        cast(nc.scalar.copy, 1, 144, HALF)
        cast(nc.vector.tensor_copy, 1, 0, CHUNK)
        cast(nc.vector.tensor_copy, 1, CHUNK, 144)
        words_out = out_1[0].rearrange("p n t -> p (n t)").bitcast(I32)
        for h in range(2):
            quantise_result(h)
            cols = slice(h * HALF, (h + 1) * HALF)
            nc.scalar.dma_start(out=words_out[:, cols], in_=out_codes[:, cols].bitcast(I32))
        for q in range(QUADS):
            queue = nc.sync if q < QUADS - 1 else nc.scalar
            queue.dma_start(
                out=out_2[0, 4 * q : 4 * q + 4, :].bitcast(I32),
                in_=out_scales[32 * q : 32 * q + 4, :].bitcast(I32),
            )
